import numpy as np
import ml_dtypes


def mxq(x, axis, fmt="e4m3"):
    dtype, down = {"e4m3": (ml_dtypes.float8_e4m3fn, 7), "e5m2": (ml_dtypes.float8_e5m2, 14)}[fmt]
    v = np.moveaxis(np.asarray(x, np.float32).astype(ml_dtypes.bfloat16).astype(np.float64), axis, -1)
    blocks = v.reshape(v.shape[:-1] + (-1, 32))
    amax = np.abs(blocks).max(-1, keepdims=True)
    byte = np.maximum(np.where(amax > 0, np.frexp(amax)[1] - 1 + 127, 0) - down, 1)
    scale = np.exp2(byte - 127.0)
    codes = (blocks / scale).astype(np.float32).astype(dtype).astype(np.float64)
    return np.moveaxis((codes * scale).reshape(v.shape), -1, axis)


WIDE = False


def mx_kscale(k):
    if not WIDE:
        return np.ones(k)
    levels = np.array([10, -10, 5, -5, 0])
    if k % 512:
        return np.exp2(np.random.permutation(np.resize(levels, k // 32))).repeat(32)
    a = np.empty((k // 512, 16))
    for p in range(k // 512):
        a[p, :8] = np.random.permutation(np.resize(levels, 8))
        for g in range(8):
            far = levels[np.abs(levels - a[p, g]) >= 10]
            a[p, g + 8] = far[np.random.randint(len(far))]
    return np.exp2(a.ravel()).repeat(32)


def f64(x):
    return np.asarray(x).astype(np.float64)


def striped(idx):
    return np.tile(idx.reshape(-1, 16).T, (8, 1)).astype(np.uint16)


def unstriped(offs):
    return offs[:16].T.reshape(-1).astype(np.int64)


def striped8(idx):
    return np.concatenate([x.reshape(-1, 16).T for x in idx]).astype(np.uint16)


def runs(offs, k):
    lists = np.stack([offs[16 * r : 16 * r + 16].T.reshape(-1) for r in range(8)]).astype(np.int64)
    return lists[np.arange(k) % 512 // 64]


def pack_weight(w):
    k, n = w.shape
    w = f64(np.asarray(w, np.float32).astype(ml_dtypes.bfloat16)).reshape(k // 32, 32, n)
    amax = np.abs(w).max(1)
    byte = np.clip(np.where(amax > 0, np.frexp(amax)[1] - 1 + 127 - 7, 1), 1, 254)
    scaled = (w * np.exp2(127.0 - byte)[:, None, :]).reshape(k, n).astype(np.float32)
    words = np.ascontiguousarray(scaled.reshape(k // 512, 128, 4, n).transpose(0, 1, 3, 2)).astype(ml_dtypes.float8_e4m3fn).view(np.uint8)
    return words, np.ascontiguousarray(byte.astype(np.uint8).reshape(k // 512, 16, n))


def unpack_weight(words, scales):
    g, p, n, _ = words.shape
    vals = np.ascontiguousarray(words).view(ml_dtypes.float8_e4m3fn).astype(np.float64) * np.repeat(np.exp2(scales.astype(np.float64) - 127.0), 8, axis=1)[..., None]
    return vals.transpose(0, 1, 3, 2).reshape(g * 512, n)


E2M1 = np.array([0.0, 0.5, 1.0, 1.5, 2.0, 3.0, 4.0, 6.0, -0.0, -0.5, -1.0, -1.5, -2.0, -3.0, -4.0, -6.0])


def pack_fp4(w):
    k, n = w.shape
    w = f64(np.asarray(w, np.float32).astype(ml_dtypes.bfloat16)).reshape(k // 32, 32, n)
    amax = np.abs(w).max(1)
    mant, ex = np.frexp(amax / 6.0)
    byte = np.clip(np.where(amax > 0, np.where(mant > 0.5, ex, ex - 1) + 127, 1), 1, 254)
    scaled = (w * np.exp2(127.0 - byte)[:, None, :]).reshape(k, n).astype(np.float32)
    c = np.ascontiguousarray(scaled.reshape(k // 512, 128, 4, n).transpose(0, 1, 3, 2)).astype(ml_dtypes.float4_e2m1fn).view(np.uint8) & 0xF
    words = (c[..., 0::2] | (c[..., 1::2] << 4)).reshape(k // 512, 128, 2 * n)
    return np.ascontiguousarray(words), np.ascontiguousarray(byte.astype(np.uint8).reshape(k // 512, 16, n))


def unpack_fp4(words, scales):
    g, _, n = scales.shape
    words = np.ascontiguousarray(words).reshape(g, 128, n, 2)
    nib = np.empty((g, 128, n, 4), np.uint8)
    nib[..., 0::2] = words & 0xF
    nib[..., 1::2] = words >> 4
    vals = E2M1[nib] * np.repeat(np.exp2(scales.astype(np.float64) - 127.0), 8, axis=1)[..., None]
    return vals.transpose(0, 1, 3, 2).reshape(g * 512, n)


def sigmoid(v):
    return 1.0 / (1.0 + np.exp(-np.maximum(v, -700.0)))

def planes(y):
    n, m = y.shape
    v = y.astype(np.float32).astype(ml_dtypes.bfloat16).astype(np.float64).reshape(n // 32, 32, m)
    top = np.abs(v).max(1)
    byte = np.clip(np.where(top > 0, np.frexp(top)[1] - 1 + 127 - 7, 1), 1, 254)
    codes = (v * np.exp2(127.0 - byte)[:, None, :]).reshape(n, m).astype(np.float32).astype(ml_dtypes.float8_e4m3fn).view(np.uint8)
    words = codes.reshape(n // 512, 128, 4, m).transpose(0, 1, 3, 2)
    return np.ascontiguousarray(words), np.ascontiguousarray(byte.astype(np.uint8).reshape(n // 512, 16, m))


K, T, S, N, H = 512, 2048, 512, 512, 512


def setup_inputs():
    n = np.random.standard_normal
    s = mx_kscale(K)[:, None]
    u = mx_kscale(H)
    packed_xT = pack_weight(n((K, T)) * s)
    packed_w1 = pack_fp4(n((K, H)) / np.sqrt(K) / s)
    packed_w2 = pack_fp4(n((H, N)) / np.sqrt(H) / u[:, None])
    return {
        "x_words": packed_xT[0],
        "x_scales": packed_xT[1],
        "w1_words": packed_w1[0],
        "w1_scales": packed_w1[1],
        "gn": (np.random.uniform(0.5, 1.5, (H, 1)) * u[:, None]).astype(np.float32),
        "w2_words": packed_w2[0],
        "w2_scales": packed_w2[1],
        "offs": striped(np.random.permutation(T)[:S]),
        "n1": striped8(np.stack([np.random.permutation(S) for _ in range(8)])),
        "n2": striped8(np.stack([np.random.permutation(S) for _ in range(8)])),
        "n3": striped8(np.stack([np.random.permutation(S) for _ in range(8)])),
    }


def reference(x_words, x_scales, w1_words, w1_scales, gn, w2_words, w2_scales, offs, n1, n2, n3):
    xq = unpack_weight(x_words, x_scales)[:, unstriped(offs)]
    y = unpack_fp4(w1_words, w1_scales).T @ xq
    sq = (y) ** 2
    z = f64(gn) * (np.sqrt(sq + 0.5 * (sq[np.arange(H)[:, None], runs(n1, H)]) + 0.25 * (sq[np.arange(H)[:, None], runs(n2, H)]) + 0.1))
    h = unpack_fp4(w2_words, w2_scales).T @ mxq(z, 0, "e4m3")
    out_0 = (h - (h[np.arange(N)[:, None], runs(n3, N)])) * sigmoid(h)
    return (out_0,) + planes(out_0)

@@ -1,0 +1,193 @@
+from contextlib import ExitStack
+
+import concourse.mybir as mybir
+
+F32 = mybir.dt.float32
+BF16 = mybir.dt.bfloat16
+I32 = mybir.dt.int32
+U32 = mybir.dt.uint32
+U16 = mybir.dt.uint16
+U8 = mybir.dt.uint8
+FP8X4 = mybir.dt.float8_e4m3fn_x4
+FP4X4 = mybir.dt.float4_e2m1fn_x4
+ACT = mybir.ActivationFunctionType
+ALU = mybir.AluOpType
+
+P = 128
+T = 2048
+S = 512
+PACK = 4
+FLOPS = 2 * 2 * 512 * 512 * 512
+HALVES = ((0, 256), (256, 512))
+SLICES = ((0, 256), (256, 384), (384, 512))
+
+
+def tile_picked_quadmean_none_po_kernel(
+    tc, x_words, x_scales, w1_words, w1_scales, gn, w2_words, w2_scales, offs, n1, n2, n3, out_0, out_1, out_2
+):
+    nc = tc.nc
+    with ExitStack() as ctx:
+        lists = ctx.enter_context(tc.tile_pool(name="lists", bufs=1))
+        sb = ctx.enter_context(tc.tile_pool(name="sb", bufs=1))
+        psum = ctx.enter_context(tc.psum_pool(name="psum", bufs=1))
+
+        def load_scale_rows(queues, plane, rows):
+            for q in range(4):
+                queues[q].dma_start(out=plane[32 * q : 32 * q + 4, :].bitcast(I32), in_=rows[0, 4 * q : 4 * q + 4, :].bitcast(I32))
+
+        def deal_words(raw, name):
+            dealt = sb.tile([P, 2 * S], U8, name=name, align_bytes=64)
+            nc.vector.tensor_copy(
+                out=dealt[:].rearrange("p (t m b) -> p t m b", t=PACK, b=2),
+                in_=raw[:].rearrange("p (m t b) -> p t m b", t=PACK, b=2),
+            )
+            return dealt
+
+        def deal_scales(engine, raw, name):
+            dealt = sb.tile([P, S], U8, name=name, align_bytes=64)
+            engine.tensor_copy(
+                out=dealt[:].rearrange("p (t m) -> p t m", t=PACK),
+                in_=raw[:].rearrange("p (m t) -> p t m", t=PACK),
+            )
+            return dealt
+
+        def entries(list_tile, a, b):
+            return list_tile[:, a // 16 : b // 16]
+
+        offs_sb = lists.tile([P, S // 16], U16, name="offs_sb")
+        n1_sb = lists.tile([P, S // 16], U16, name="n1_sb")
+        n2_sb = lists.tile([P, S // 16], U16, name="n2_sb")
+        n3_sb = lists.tile([P, S // 16], U16, name="n3_sb")
+        xw = sb.tile([P, T], I32, name="xw", align_bytes=64)
+        xs = sb.tile([P, T], U8, name="xs", tag="raw_scales", align_bytes=64)
+        w1w = sb.tile([P, 2 * S], U8, name="w1w", tag="raw_words", align_bytes=64)
+        w1s = sb.tile([P, S], U8, name="w1s", align_bytes=64)
+        gain = sb.tile([P, PACK], F32, name="gain")
+        one = sb.tile([P, 1], F32, name="one")
+        warm = sb.tile([P, 1], F32, name="warm")
+
+        nc.vector.memset(xs[:].bitcast(I32), 0)
+        nc.vector.memset(w1s[:].bitcast(I32), 0)
+        nc.vector.memset(one[:], 1.0)
+
+        nc.sync.dma_start(offs_sb[:], offs)
+        nc.sync.dma_start(n2_sb[:], n2)
+        nc.sync.dma_start(n1_sb[:], n1)
+        nc.sync.dma_start(n3_sb[:], n3)
+        nc.sync.dma_start(out=xw[:], in_=x_words[0].rearrange("p n t -> p (n t)").bitcast(I32))
+        nc.scalar.dma_start(out=w1w[:].bitcast(I32), in_=w1_words[0].bitcast(I32))
+        load_scale_rows([nc.scalar] * 4, xs, x_scales)
+        load_scale_rows([nc.gpsimd] + [nc.scalar] * 3, w1s, w1_scales)
+        nc.scalar.activation(warm[:], one[:], ACT.Sqrt)
+        nc.gpsimd.dma_start(out=gain[:], in_=gn.rearrange("(p t) o -> p (t o)", t=PACK))
+
+        w1_codes = deal_words(w1w, "w1_codes")
+        picked_scales = sb.tile([P, S], U8, name="picked_scales", align_bytes=64)
+        nc.vector.tensor_copy(picked_scales[:], xs[:].indirect(offs_sb[:]))
+        w1_bytes = deal_scales(nc.gpsimd, w1s, "w1_bytes")
+        picked_words = sb.tile([P, S], I32, name="picked_words", align_bytes=64)
+        nc.vector.tensor_copy(picked_words[:].bitcast(U32), xw[:].bitcast(U32).indirect(offs_sb[:]))
+        w2w = sb.tile([P, 2 * S], U8, name="w2w", tag="raw_words", align_bytes=64)
+        nc.sync.dma_start(out=w2w[:].bitcast(I32), in_=w2_words[0].bitcast(I32))
+        w2s = sb.tile([P, S], U8, name="w2s", tag="raw_scales", align_bytes=64)
+        nc.gpsimd.memset(w2s[:].bitcast(I32), 0)
+        load_scale_rows([nc.sync] * 4, w2s, w2_scales)
+        w2_codes = deal_words(w2w, "w2_codes")
+        w2_bytes = deal_scales(nc.vector, w2s, "w2_bytes")
+
+        def product(out, codes, scale_bytes, t, rhs, rhs_scale):
+            nc.tensor.matmul_mx(
+                out=out,
+                lhsT=codes[:, 2 * P * t : 2 * P * (t + 1)].bitcast(FP4X4),
+                lhsT_scale=scale_bytes[:, P * t : P * (t + 1)],
+                rhs=rhs.bitcast(FP8X4),
+                rhs_scale=rhs_scale,
+                start=True,
+                stop=True,
+            )
+
+        part = sb.tile([P, PACK, S], F32, name="part")
+        total = sb.tile([P, PACK, S], F32, name="total", tag="total_then_gate")
+        root = sb.tile([P, PACK, S], F32, name="root")
+        own = sb.tile([P, PACK, S], F32, name="own")
+        z_bf = sb.tile([P, S * PACK], BF16, name="z_bf", align_bytes=64)
+        z_codes = sb.tile([P, S], I32, name="z_codes", align_bytes=64)
+        z_scales = sb.tile([P, S], U8, name="z_scales", align_bytes=64)
+        h_win = [sb.tile([P, S], F32, name=f"h_win{t}") for t in range(PACK)]
+        h_own = sb.tile([P, PACK, S], F32, name="h_own")
+        h_banks = []
+
+        z_planes = sb.tile([P, PACK, S], BF16, name="z_planes", align_bytes=64)
+
+        def woven(tile, a, b):
+            return tile[:, PACK * a : PACK * b].rearrange("p (c i t) -> p c t i", i=4, t=PACK)
+
+        def by_plane(tile, a, b):
+            return tile[:, :, a:b].rearrange("p t (c i) -> p c t i", i=4)
+
+        windows = []
+        for t in range(PACK):
+            y = psum.tile([P, S], F32, name=f"y{t}")
+            product(y[:], w1_codes, w1_bytes, t, picked_words[:], picked_scales[:])
+            sq1 = sb.tile([P, S], F32, name=f"sq1_{t}")
+            sq2 = sb.tile([P, S], F32, name=f"sq2_{t}")
+            nc.scalar.activation(sq1[:], y[:], ACT.Square)
+            nc.scalar.activation(own[:, t, :], y[:], ACT.Square, scale=2.0)
+            nc.scalar.activation(sq2[:], y[:], ACT.Square, scale=2.0**0.5)
+            windows.append((sq1, sq2))
+
+        for t in range(PACK):
+            sq1, sq2 = windows[t]
+            pieces = HALVES if t < PACK - 1 else SLICES
+            for a, b in pieces:
+                nc.vector.tensor_tensor(part[:, t, a:b], sq1[:].indirect(entries(n2_sb, a, b)), own[:, t, a:b], ALU.add)
+            for a, b in pieces:
+                nc.vector.tensor_tensor(total[:, t, a:b], sq2[:].indirect(entries(n1_sb, a, b)), part[:, t, a:b], ALU.add)
+            for a, b in ((0, S),) if t < PACK - 1 else SLICES:
+                nc.scalar.activation(root[:, t, a:b], total[:, t, a:b], ACT.Sqrt, scale=0.25, bias=0.1)
+                nc.scalar.activation(z_planes[:, t, a:b], root[:, t, a:b], ACT.Copy, scale=gain[:, t : t + 1])
+
+        gate = sb.tile([P, PACK, S], F32, name="gate", tag="total_then_gate")
+        nc.scalar.activation(gate[:, 0, 0:1], one[:], ACT.Sigmoid)
+
+        for a, b in SLICES:
+            width = b - a
+            nc.vector.tensor_copy(woven(z_bf, a, b), by_plane(z_planes, a, b))
+            nc.vector.quantize_mx(out=z_codes[:, a:b].bitcast(FP8X4), scales=z_scales[:, a:b], in_=z_bf[:, PACK * a : PACK * b])
+            per_bank = S // width
+            for t0 in range(0, PACK, per_bank):
+                bank = psum.tile([P, per_bank, width], F32, name=f"h_{a}_{t0}")
+                for t in range(t0, t0 + per_bank):
+                    product(bank[:, t - t0, :], w2_codes, w2_bytes, t, z_codes[:, a:b], z_scales[:, a:b])
+                for t in range(t0, t0 + per_bank):
+                    nc.scalar.copy(h_win[t][:, a:b], bank[:, t - t0, :])
+                h_banks.append((bank, t0, per_bank, a, b))
+
+        for bank, t0, per_bank, a, b in h_banks:
+            if a == 0:
+                nc.vector.tensor_copy(h_own[:, t0 : t0 + per_bank, a:b], bank[:])
+            else:
+                nc.scalar.copy(h_own[:, t0 : t0 + per_bank, a:b], bank[:])
+            nc.scalar.activation(gate[:, t0 : t0 + per_bank, a:b], bank[:], ACT.Sigmoid)
+
+        diff = sb.tile([P, PACK, S], F32, name="diff")
+        res = sb.tile([P, PACK, S], F32, name="res")
+        res_bf = sb.tile([P, S * PACK], BF16, name="res_bf", align_bytes=64)
+        res_codes = sb.tile([P, S], I32, name="res_codes", align_bytes=64)
+        res_scales = sb.tile([P, S], U8, name="res_scales", align_bytes=64)
+        out_rows = out_0.rearrange("(p t) j -> p t j", t=PACK)
+        out_words = out_1[0].rearrange("p j t -> p (j t)").bitcast(I32)
+        for a, b in SLICES:
+            for t in range(PACK):
+                nc.vector.tensor_tensor(diff[:, t, a:b], h_win[t][:].indirect(entries(n3_sb, a, b)), h_own[:, t, a:b], ALU.subtract)
+            nc.vector.scalar_tensor_tensor(res[:, :, a:b], diff[:, :, a:b], -1.0, gate[:, :, a:b], ALU.mult, ALU.mult)
+            nc.sync.dma_start(out=out_rows[:, :, a:b], in_=res[:, :, a:b])
+            if b < S:
+                nc.scalar.copy(woven(res_bf, a, b), by_plane(res, a, b))
+            else:
+                nc.vector.tensor_copy(woven(res_bf, a, b), by_plane(res, a, b))
+            nc.vector.quantize_mx(out=res_codes[:, a:b].bitcast(FP8X4), scales=res_scales[:, a:b], in_=res_bf[:, PACK * a : PACK * b])
+            nc.sync.dma_start(out=out_words[:, a:b], in_=res_codes[:, a:b])
+        for q in range(4):
+            queue = nc.sync if q % 2 else nc.scalar
+            queue.dma_start(out=out_2[0, 4 * q : 4 * q + 4, :].bitcast(I32), in_=res_scales[32 * q : 32 * q + 4, :].bitcast(I32))

@@ -59,26 +59,31 @@ def tile_picked_quadmean_none_po_kernel(
         n2_sb = lists.tile([P, S // 16], U16, name="n2_sb")
         n3_sb = lists.tile([P, S // 16], U16, name="n3_sb")
         xw = sb.tile([P, T], I32, name="xw", align_bytes=64)
-        xs = sb.tile([P, T], U8, name="xs", tag="raw_scales", align_bytes=64)
-        w1w = sb.tile([P, 2 * S], U8, name="w1w", tag="raw_words", align_bytes=64)
+        xs = sb.tile([P, T], U8, name="xs", align_bytes=64)
+        w1w = sb.tile([P, 2 * S], U8, name="w1w", align_bytes=64)
         w1s = sb.tile([P, S], U8, name="w1s", align_bytes=64)
         gain = sb.tile([P, PACK], F32, name="gain")
         one = sb.tile([P, 1], F32, name="one")
         warm = sb.tile([P, 1], F32, name="warm")
 
+        w2w = sb.tile([P, 2 * S], U8, name="w2w", align_bytes=64)
+        w2s = sb.tile([P, S], U8, name="w2s", align_bytes=64)
         nc.vector.memset(xs[:].bitcast(I32), 0)
         nc.vector.memset(w1s[:].bitcast(I32), 0)
         nc.vector.memset(one[:], 1.0)
+        nc.vector.memset(w2s[:].bitcast(I32), 0)
 
         nc.sync.dma_start(offs_sb[:], offs)
+        nc.scalar.dma_start(out=w1w[:].bitcast(I32), in_=w1_words[0].bitcast(I32))
         nc.sync.dma_start(n2_sb[:], n2)
+        load_scale_rows([nc.sync, nc.scalar] * 2, xs, x_scales)
+        nc.sync.dma_start(out=xw[:], in_=x_words[0].rearrange("p n t -> p (n t)").bitcast(I32))
+        load_scale_rows([nc.sync] * 4, w1s, w1_scales)
+        nc.scalar.activation(warm[:], one[:], ACT.Sqrt)
         nc.sync.dma_start(n1_sb[:], n1)
         nc.sync.dma_start(n3_sb[:], n3)
-        nc.sync.dma_start(out=xw[:], in_=x_words[0].rearrange("p n t -> p (n t)").bitcast(I32))
-        nc.scalar.dma_start(out=w1w[:].bitcast(I32), in_=w1_words[0].bitcast(I32))
-        load_scale_rows([nc.scalar] * 4, xs, x_scales)
-        load_scale_rows([nc.gpsimd] + [nc.scalar] * 3, w1s, w1_scales)
-        nc.scalar.activation(warm[:], one[:], ACT.Sqrt)
+        nc.sync.dma_start(out=w2w[:].bitcast(I32), in_=w2_words[0].bitcast(I32))
+        load_scale_rows([nc.sync] * 4, w2s, w2_scales)
         nc.gpsimd.dma_start(out=gain[:], in_=gn.rearrange("(p t) o -> p (t o)", t=PACK))
 
         w1_codes = deal_words(w1w, "w1_codes")
@@ -86,14 +91,10 @@ def tile_picked_quadmean_none_po_kernel(
         nc.vector.tensor_copy(picked_scales[:], xs[:].indirect(offs_sb[:]))
         w1_bytes = deal_scales(nc.gpsimd, w1s, "w1_bytes")
         picked_words = sb.tile([P, S], I32, name="picked_words", align_bytes=64)
-        nc.vector.tensor_copy(picked_words[:].bitcast(U32), xw[:].bitcast(U32).indirect(offs_sb[:]))
-        w2w = sb.tile([P, 2 * S], U8, name="w2w", tag="raw_words", align_bytes=64)
-        nc.sync.dma_start(out=w2w[:].bitcast(I32), in_=w2_words[0].bitcast(I32))
-        w2s = sb.tile([P, S], U8, name="w2s", tag="raw_scales", align_bytes=64)
-        nc.gpsimd.memset(w2s[:].bitcast(I32), 0)
-        load_scale_rows([nc.sync] * 4, w2s, w2_scales)
+        for a, b in HALVES:
+            nc.vector.tensor_copy(picked_words[:, a:b].bitcast(U32), xw[:].bitcast(U32).indirect(entries(offs_sb, a, b)))
         w2_codes = deal_words(w2w, "w2_codes")
-        w2_bytes = deal_scales(nc.vector, w2s, "w2_bytes")
+        w2_bytes = deal_scales(nc.gpsimd, w2s, "w2_bytes")
 
         def product(out, codes, scale_bytes, t, rhs, rhs_scale):
             nc.tensor.matmul_mx(
@@ -115,9 +116,8 @@ def tile_picked_quadmean_none_po_kernel(
         z_scales = sb.tile([P, S], U8, name="z_scales", align_bytes=64)
         h_win = [sb.tile([P, S], F32, name=f"h_win{t}") for t in range(PACK)]
         h_own = sb.tile([P, PACK, S], F32, name="h_own")
-        h_banks = []
 
-        z_planes = sb.tile([P, PACK, S], BF16, name="z_planes", align_bytes=64)
+        z_planes = sb.tile([P, PACK, 256], BF16, name="z_planes", align_bytes=64)
 
         def woven(tile, a, b):
             return tile[:, PACK * a : PACK * b].rearrange("p (c i t) -> p c t i", i=4, t=PACK)
@@ -125,50 +125,69 @@ def tile_picked_quadmean_none_po_kernel(
         def by_plane(tile, a, b):
             return tile[:, :, a:b].rearrange("p t (c i) -> p c t i", i=4)
 
+        half = S // 2
         windows = []
         for t in range(PACK):
-            y = psum.tile([P, S], F32, name=f"y{t}")
-            product(y[:], w1_codes, w1_bytes, t, picked_words[:], picked_scales[:])
             sq1 = sb.tile([P, S], F32, name=f"sq1_{t}")
             sq2 = sb.tile([P, S], F32, name=f"sq2_{t}")
-            nc.scalar.activation(sq1[:], y[:], ACT.Square)
-            nc.scalar.activation(own[:, t, :], y[:], ACT.Square, scale=2.0)
-            nc.scalar.activation(sq2[:], y[:], ACT.Square, scale=2.0**0.5)
+            for a, b in HALVES if t == 0 else ((0, S),):
+                y = psum.tile([P, b - a], F32, name=f"y{t}_{a}", tag=f"bank{t + (b == S)}")
+                product(y[:], w1_codes, w1_bytes, t, picked_words[:, a:b], picked_scales[:, a:b])
+                nc.scalar.activation(sq1[:, a:b], y[:], ACT.Square)
+                nc.scalar.activation(own[:, t, a:b], y[:], ACT.Square, scale=2.0)
+                nc.scalar.activation(sq2[:, a:b], y[:], ACT.Square, scale=2.0**0.5)
             windows.append((sq1, sq2))
 
         for t in range(PACK):
             sq1, sq2 = windows[t]
-            pieces = HALVES if t < PACK - 1 else SLICES
-            for a, b in pieces:
+            for a, b in HALVES:
                 nc.vector.tensor_tensor(part[:, t, a:b], sq1[:].indirect(entries(n2_sb, a, b)), own[:, t, a:b], ALU.add)
-            for a, b in pieces:
+            for a, b in HALVES:
                 nc.vector.tensor_tensor(total[:, t, a:b], sq2[:].indirect(entries(n1_sb, a, b)), part[:, t, a:b], ALU.add)
-            for a, b in ((0, S),) if t < PACK - 1 else SLICES:
-                nc.scalar.activation(root[:, t, a:b], total[:, t, a:b], ACT.Sqrt, scale=0.25, bias=0.1)
-                nc.scalar.activation(z_planes[:, t, a:b], root[:, t, a:b], ACT.Copy, scale=gain[:, t : t + 1])
+
+        def take_root(t0, t1, a, b):
+            nc.scalar.activation(root[:, t0:t1, a:b], total[:, t0:t1, a:b], ACT.Sqrt, scale=0.25, bias=0.1)
+
+        def apply_gain(t):
+            nc.scalar.activation(z_planes[:, t, :], root[:, t, half:S], ACT.Copy, scale=gain[:, t : t + 1])
+
+        take_root(0, 2, 0, S)
+        take_root(2, 3, 0, S)
+        apply_gain(0)
+        apply_gain(1)
+        take_root(3, 4, 0, half)
+        apply_gain(2)
+        take_root(3, 4, half, S)
+        apply_gain(3)
 
         gate = sb.tile([P, PACK, S], F32, name="gate", tag="total_then_gate")
         nc.scalar.activation(gate[:, 0, 0:1], one[:], ACT.Sigmoid)
 
-        for a, b in SLICES:
-            width = b - a
-            nc.vector.tensor_copy(woven(z_bf, a, b), by_plane(z_planes, a, b))
+        spread = gain[:].unsqueeze(1).unsqueeze(3).to_broadcast([P, half // 4, PACK, 4])
+        nc.vector.tensor_tensor(woven(z_bf, 0, half), by_plane(root, 0, half), spread, ALU.mult)
+        nc.vector.tensor_copy(woven(z_bf, half, S), by_plane(z_planes, 0, half))
+        banks = {}
+        for a, b in HALVES:
             nc.vector.quantize_mx(out=z_codes[:, a:b].bitcast(FP8X4), scales=z_scales[:, a:b], in_=z_bf[:, PACK * a : PACK * b])
-            per_bank = S // width
-            for t0 in range(0, PACK, per_bank):
-                bank = psum.tile([P, per_bank, width], F32, name=f"h_{a}_{t0}")
-                for t in range(t0, t0 + per_bank):
+        for t0 in (0, 2):
+            for a, b in HALVES:
+                bank = psum.tile([P, 2, half], F32, name=f"h_{a}_{t0}", tag=f"bank{(5 + t0 // 2 + 2 * (a > 0)) % 8}")
+                for t in (t0, t0 + 1):
                     product(bank[:, t - t0, :], w2_codes, w2_bytes, t, z_codes[:, a:b], z_scales[:, a:b])
-                for t in range(t0, t0 + per_bank):
-                    nc.scalar.copy(h_win[t][:, a:b], bank[:, t - t0, :])
-                h_banks.append((bank, t0, per_bank, a, b))
+                banks[a, t0] = bank
 
-        for bank, t0, per_bank, a, b in h_banks:
-            if a == 0:
-                nc.vector.tensor_copy(h_own[:, t0 : t0 + per_bank, a:b], bank[:])
-            else:
-                nc.scalar.copy(h_own[:, t0 : t0 + per_bank, a:b], bank[:])
-            nc.scalar.activation(gate[:, t0 : t0 + per_bank, a:b], bank[:], ACT.Sigmoid)
+        nc.vector.tensor_copy(h_win[0][:, 0:half], banks[0, 0][:, 0, :])
+        nc.vector.tensor_copy(h_own[:, 0:2, 0:half], banks[0, 0][:])
+        nc.vector.tensor_copy(h_win[1][:, 0:half], banks[0, 0][:, 1, :])
+        for t in range(PACK):
+            if t >= 2:
+                nc.scalar.copy(h_win[t][:, 0:half], banks[0, 2][:, t - 2, :])
+            nc.scalar.copy(h_win[t][:, half:S], banks[half, t - t % 2][:, t % 2, :])
+            nc.sync.dma_start(out=h_own[:, t, half:S], in_=h_win[t][:, half:S])
+            if t == 2:
+                nc.scalar.copy(h_own[:, 2:4, 0:half], banks[0, 2][:])
+        for a, b in SLICES:
+            nc.scalar.activation(gate[:, :, a:b], h_own[:, :, a:b], ACT.Sigmoid)
 
         diff = sb.tile([P, PACK, S], F32, name="diff")
         res = sb.tile([P, PACK, S], F32, name="res")

@@ -17,6 +17,7 @@ P = 128
 T = 2048
 S = 512
 PACK = 4
+X_FIRST = 1536
 FLOPS = 2 * 2 * 512 * 512 * 512
 HALVES = ((0, 256), (256, 512))
 SLICES = ((0, 256), (256, 384), (384, 512))
@@ -43,9 +44,9 @@ def tile_picked_quadmean_none_po_kernel(
             )
             return dealt
 
-        def deal_scales(engine, raw, name):
+        def deal_scales(raw, name):
             dealt = sb.tile([P, S], U8, name=name, align_bytes=64)
-            engine.tensor_copy(
+            nc.vector.tensor_copy(
                 out=dealt[:].rearrange("p (t m) -> p t m", t=PACK),
                 in_=raw[:].rearrange("p (m t) -> p t m", t=PACK),
             )
@@ -73,28 +74,30 @@ def tile_picked_quadmean_none_po_kernel(
         nc.vector.memset(one[:], 1.0)
         nc.vector.memset(w2s[:].bitcast(I32), 0)
 
+        x_rows = x_words[0].rearrange("p n t -> p (n t)").bitcast(I32)
         nc.sync.dma_start(offs_sb[:], offs)
         nc.scalar.dma_start(out=w1w[:].bitcast(I32), in_=w1_words[0].bitcast(I32))
         nc.sync.dma_start(n2_sb[:], n2)
         load_scale_rows([nc.sync, nc.scalar] * 2, xs, x_scales)
-        nc.sync.dma_start(out=xw[:], in_=x_words[0].rearrange("p n t -> p (n t)").bitcast(I32))
+        nc.sync.dma_start(out=xw[:, 0:X_FIRST], in_=x_rows[:, 0:X_FIRST])
         load_scale_rows([nc.sync] * 4, w1s, w1_scales)
+        nc.sync.dma_start(out=xw[:, X_FIRST:T], in_=x_rows[:, X_FIRST:T])
         nc.scalar.activation(warm[:], one[:], ACT.Sqrt)
-        nc.sync.dma_start(n1_sb[:], n1)
-        nc.sync.dma_start(n3_sb[:], n3)
         nc.sync.dma_start(out=w2w[:].bitcast(I32), in_=w2_words[0].bitcast(I32))
         load_scale_rows([nc.sync] * 4, w2s, w2_scales)
-        nc.gpsimd.dma_start(out=gain[:], in_=gn.rearrange("(p t) o -> p (t o)", t=PACK))
+        nc.sync.dma_start(n1_sb[:], n1)
+        nc.sync.dma_start(n3_sb[:], n3)
+        nc.sync.dma_start(out=gain[:], in_=gn.rearrange("(p t) o -> p (t o)", t=PACK))
 
         w1_codes = deal_words(w1w, "w1_codes")
         picked_scales = sb.tile([P, S], U8, name="picked_scales", align_bytes=64)
         nc.vector.tensor_copy(picked_scales[:], xs[:].indirect(offs_sb[:]))
-        w1_bytes = deal_scales(nc.gpsimd, w1s, "w1_bytes")
+        w1_bytes = deal_scales(w1s, "w1_bytes")
         picked_words = sb.tile([P, S], I32, name="picked_words", align_bytes=64)
         for a, b in HALVES:
             nc.vector.tensor_copy(picked_words[:, a:b].bitcast(U32), xw[:].bitcast(U32).indirect(entries(offs_sb, a, b)))
         w2_codes = deal_words(w2w, "w2_codes")
-        w2_bytes = deal_scales(nc.gpsimd, w2s, "w2_bytes")
+        w2_bytes = deal_scales(w2s, "w2_bytes")
 
         def product(out, codes, scale_bytes, t, rhs, rhs_scale):
             nc.tensor.matmul_mx(
@@ -117,7 +120,7 @@ def tile_picked_quadmean_none_po_kernel(
         h_win = [sb.tile([P, S], F32, name=f"h_win{t}") for t in range(PACK)]
         h_own = sb.tile([P, PACK, S], F32, name="h_own")
 
-        z_planes = sb.tile([P, PACK, 256], BF16, name="z_planes", align_bytes=64)
+        z_planes = sb.tile([P, PACK, S], BF16, name="z_planes", align_bytes=64)
 
         def woven(tile, a, b):
             return tile[:, PACK * a : PACK * b].rearrange("p (c i t) -> p c t i", i=4, t=PACK)
@@ -135,7 +138,10 @@ def tile_picked_quadmean_none_po_kernel(
                 product(y[:], w1_codes, w1_bytes, t, picked_words[:, a:b], picked_scales[:, a:b])
                 nc.scalar.activation(sq1[:, a:b], y[:], ACT.Square)
                 nc.scalar.activation(own[:, t, a:b], y[:], ACT.Square, scale=2.0)
-                nc.scalar.activation(sq2[:, a:b], y[:], ACT.Square, scale=2.0**0.5)
+            if t == 0:
+                nc.scalar.activation(sq2[:], sq1[:], ACT.Copy, scale=2.0)
+            else:
+                nc.scalar.activation(sq2[:], y[:], ACT.Square, scale=2.0**0.5)
             windows.append((sq1, sq2))
 
         for t in range(PACK):
@@ -148,24 +154,28 @@ def tile_picked_quadmean_none_po_kernel(
         def take_root(t0, t1, a, b):
             nc.scalar.activation(root[:, t0:t1, a:b], total[:, t0:t1, a:b], ACT.Sqrt, scale=0.25, bias=0.1)
 
-        def apply_gain(t):
-            nc.scalar.activation(z_planes[:, t, :], root[:, t, half:S], ACT.Copy, scale=gain[:, t : t + 1])
+        def gain_on_scalar(t, a, b):
+            nc.scalar.activation(z_planes[:, t, a:b], root[:, t, a:b], ACT.Copy, scale=gain[:, t : t + 1])
+
+        def gain_on_vector(t, a, b):
+            nc.vector.tensor_scalar(z_planes[:, t, a:b], root[:, t, a:b], gain[:, t : t + 1], None, ALU.mult)
 
         take_root(0, 2, 0, S)
         take_root(2, 3, 0, S)
-        apply_gain(0)
-        apply_gain(1)
+        gain_on_scalar(0, 0, S)
+        gain_on_scalar(1, 0, S)
+        gain_on_vector(2, 0, half)
         take_root(3, 4, 0, half)
-        apply_gain(2)
+        gain_on_vector(3, 0, half)
+        gain_on_scalar(2, half, S)
         take_root(3, 4, half, S)
-        apply_gain(3)
+        gain_on_scalar(3, half, S)
 
         gate = sb.tile([P, PACK, S], F32, name="gate", tag="total_then_gate")
         nc.scalar.activation(gate[:, 0, 0:1], one[:], ACT.Sigmoid)
 
-        spread = gain[:].unsqueeze(1).unsqueeze(3).to_broadcast([P, half // 4, PACK, 4])
-        nc.vector.tensor_tensor(woven(z_bf, 0, half), by_plane(root, 0, half), spread, ALU.mult)
-        nc.vector.tensor_copy(woven(z_bf, half, S), by_plane(z_planes, 0, half))
+        for a, b in HALVES:
+            nc.vector.tensor_copy(woven(z_bf, a, b), by_plane(z_planes, a, b))
         banks = {}
         for a, b in HALVES:
             nc.vector.quantize_mx(out=z_codes[:, a:b].bitcast(FP8X4), scales=z_scales[:, a:b], in_=z_bf[:, PACK * a : PACK * b])
@@ -202,7 +212,10 @@ def tile_picked_quadmean_none_po_kernel(
             nc.vector.scalar_tensor_tensor(res[:, :, a:b], diff[:, :, a:b], -1.0, gate[:, :, a:b], ALU.mult, ALU.mult)
             nc.sync.dma_start(out=out_rows[:, :, a:b], in_=res[:, :, a:b])
             if b < S:
-                nc.scalar.copy(woven(res_bf, a, b), by_plane(res, a, b))
+                nc.scalar.copy(
+                    res_bf[:, PACK * a : PACK * b].rearrange("p (j t) -> p j t", t=PACK),
+                    res[:, :, a:b].rearrange("p t j -> p j t"),
+                )
             else:
                 nc.vector.tensor_copy(woven(res_bf, a, b), by_plane(res, a, b))
             nc.vector.quantize_mx(out=res_codes[:, a:b].bitcast(FP8X4), scales=res_scales[:, a:b], in_=res_bf[:, PACK * a : PACK * b])

@@ -68,7 +68,7 @@ def tile_picked_quadmean_none_po_kernel(
         warm = sb.tile([P, 1], F32, name="warm")
 
         w2w = sb.tile([P, 2 * S], U8, name="w2w", align_bytes=64)
-        w2s = sb.tile([P, S], U8, name="w2s", align_bytes=64)
+        w2s = sb.tile([P, S], U8, name="w2s", tag="w2s_then_part", align_bytes=64)
         nc.vector.memset(xs[:].bitcast(I32), 0)
         nc.vector.memset(w1s[:].bitcast(I32), 0)
         nc.vector.memset(one[:], 1.0)
@@ -110,11 +110,10 @@ def tile_picked_quadmean_none_po_kernel(
                 stop=True,
             )
 
-        part = sb.tile([P, PACK, S], F32, name="part")
+        part = sb.tile([P, PACK, S], F32, name="part", tag="w2s_then_part", align_bytes=64)
         total = sb.tile([P, PACK, S], F32, name="total", tag="total_then_gate")
         root = sb.tile([P, PACK, S], F32, name="root")
         own = sb.tile([P, PACK, S], F32, name="own")
-        z_bf = sb.tile([P, S * PACK], BF16, name="z_bf", align_bytes=64)
         z_codes = sb.tile([P, S], I32, name="z_codes", align_bytes=64)
         z_scales = sb.tile([P, S], U8, name="z_scales", align_bytes=64)
         h_win = [sb.tile([P, S], F32, name=f"h_win{t}") for t in range(PACK)]
@@ -162,40 +161,44 @@ def tile_picked_quadmean_none_po_kernel(
 
         take_root(0, 2, 0, S)
         take_root(2, 3, 0, S)
-        gain_on_scalar(0, 0, S)
-        gain_on_scalar(1, 0, S)
+        gain_on_scalar(0, 0, half)
+        gain_on_scalar(1, 0, half)
         gain_on_vector(2, 0, half)
         take_root(3, 4, 0, half)
         gain_on_vector(3, 0, half)
-        gain_on_scalar(2, half, S)
+        gain_on_scalar(0, half, S)
+        gain_on_scalar(1, half, S)
         take_root(3, 4, half, S)
-        gain_on_scalar(3, half, S)
+        gain_on_scalar(2, half, S)
+        gain_on_vector(3, half, S)
 
         gate = sb.tile([P, PACK, S], F32, name="gate", tag="total_then_gate")
         nc.scalar.activation(gate[:, 0, 0:1], one[:], ACT.Sigmoid)
 
-        for a, b in HALVES:
-            nc.vector.tensor_copy(woven(z_bf, a, b), by_plane(z_planes, a, b))
-        banks = {}
-        for a, b in HALVES:
-            nc.vector.quantize_mx(out=z_codes[:, a:b].bitcast(FP8X4), scales=z_scales[:, a:b], in_=z_bf[:, PACK * a : PACK * b])
-        for t0 in (0, 2):
-            for a, b in HALVES:
-                bank = psum.tile([P, 2, half], F32, name=f"h_{a}_{t0}", tag=f"bank{(5 + t0 // 2 + 2 * (a > 0)) % 8}")
-                for t in (t0, t0 + 1):
-                    product(bank[:, t - t0, :], w2_codes, w2_bytes, t, z_codes[:, a:b], z_scales[:, a:b])
-                banks[a, t0] = bank
+        quarter = S // 4
+        for a in range(0, S, quarter):
+            b = a + quarter
+            z_bf = sb.tile([P, quarter * PACK], BF16, name="z_bf", bufs=2, align_bytes=64)
+            nc.vector.tensor_copy(woven(z_bf, 0, quarter), by_plane(z_planes, a, b))
+            nc.vector.quantize_mx(out=z_codes[:, a:b].bitcast(FP8X4), scales=z_scales[:, a:b], in_=z_bf[:])
 
-        nc.vector.tensor_copy(h_win[0][:, 0:half], banks[0, 0][:, 0, :])
-        nc.vector.tensor_copy(h_own[:, 0:2, 0:half], banks[0, 0][:])
-        nc.vector.tensor_copy(h_win[1][:, 0:half], banks[0, 0][:, 1, :])
+        def second_product(out, t, a, b):
+            product(out, w2_codes, w2_bytes, t, z_codes[:, a:b], z_scales[:, a:b])
+
+        first = psum.tile([P, 2, half], F32, name="h_first", tag="bank5")
+        for t in (0, 1):
+            second_product(first[:, t, :], t, 0, half)
+        nc.vector.tensor_copy(h_win[0][:, 0:half], first[:, 0, :])
+        nc.vector.tensor_copy(h_own[:, 0:2, 0:half], first[:])
+        nc.vector.tensor_copy(h_win[1][:, 0:half], first[:, 1, :])
         for t in range(PACK):
-            if t >= 2:
-                nc.scalar.copy(h_win[t][:, 0:half], banks[0, 2][:, t - 2, :])
-            nc.scalar.copy(h_win[t][:, half:S], banks[half, t - t % 2][:, t % 2, :])
+            a = half if t < 2 else 0
+            bank = psum.tile([P, S - a], F32, name=f"h_rest{t}", tag=f"bank{(6 + t) % 8}")
+            second_product(bank[:], t, a, S)
+            nc.scalar.copy(h_win[t][:, a:S], bank[:])
             nc.sync.dma_start(out=h_own[:, t, half:S], in_=h_win[t][:, half:S])
-            if t == 2:
-                nc.scalar.copy(h_own[:, 2:4, 0:half], banks[0, 2][:])
+            if t >= 2:
+                nc.scalar.copy(h_own[:, t, 0:half], bank[:, 0:half])
         for a, b in SLICES:
             nc.scalar.activation(gate[:, :, a:b], h_own[:, :, a:b], ACT.Sigmoid)
 
@@ -209,7 +212,9 @@ def tile_picked_quadmean_none_po_kernel(
         for a, b in SLICES:
             for t in range(PACK):
                 nc.vector.tensor_tensor(diff[:, t, a:b], h_win[t][:].indirect(entries(n3_sb, a, b)), h_own[:, t, a:b], ALU.subtract)
-            nc.vector.scalar_tensor_tensor(res[:, :, a:b], diff[:, :, a:b], -1.0, gate[:, :, a:b], ALU.mult, ALU.mult)
+            pieces = ((a, b),) if b < S else ((a, (a + b) // 2), ((a + b) // 2, b))
+            for c, d in pieces:
+                nc.vector.scalar_tensor_tensor(res[:, :, c:d], diff[:, :, c:d], -1.0, gate[:, :, c:d], ALU.mult, ALU.mult)
             nc.sync.dma_start(out=out_rows[:, :, a:b], in_=res[:, :, a:b])
             if b < S:
                 nc.scalar.copy(
@@ -217,7 +222,8 @@ def tile_picked_quadmean_none_po_kernel(
                     res[:, :, a:b].rearrange("p t j -> p j t"),
                 )
             else:
-                nc.vector.tensor_copy(woven(res_bf, a, b), by_plane(res, a, b))
+                for c, d in pieces:
+                    nc.vector.tensor_copy(woven(res_bf, c, d), by_plane(res, c, d))
             nc.vector.quantize_mx(out=res_codes[:, a:b].bitcast(FP8X4), scales=res_scales[:, a:b], in_=res_bf[:, PACK * a : PACK * b])
             nc.sync.dma_start(out=out_words[:, a:b], in_=res_codes[:, a:b])
         for q in range(4):

from contextlib import ExitStack

import concourse.mybir as mybir

F32 = mybir.dt.float32
BF16 = mybir.dt.bfloat16
I32 = mybir.dt.int32
U32 = mybir.dt.uint32
U16 = mybir.dt.uint16
U8 = mybir.dt.uint8
FP8X4 = mybir.dt.float8_e4m3fn_x4
FP4X4 = mybir.dt.float4_e2m1fn_x4
ACT = mybir.ActivationFunctionType
ALU = mybir.AluOpType

P = 128
T = 2048
S = 512
PACK = 4
X_FIRST = 1536
FLOPS = 2 * 2 * 512 * 512 * 512
HALVES = ((0, 256), (256, 512))
SLICES = ((0, 256), (256, 384), (384, 512))


def tile_picked_quadmean_none_po_kernel(
    tc, x_words, x_scales, w1_words, w1_scales, gn, w2_words, w2_scales, offs, n1, n2, n3, out_0, out_1, out_2
):
    nc = tc.nc
    with ExitStack() as ctx:
        lists = ctx.enter_context(tc.tile_pool(name="lists", bufs=1))
        sb = ctx.enter_context(tc.tile_pool(name="sb", bufs=1))
        psum = ctx.enter_context(tc.psum_pool(name="psum", bufs=1))

        def load_scale_rows(queues, plane, rows):
            for q in range(4):
                queues[q].dma_start(out=plane[32 * q : 32 * q + 4, :].bitcast(I32), in_=rows[0, 4 * q : 4 * q + 4, :].bitcast(I32))

        def deal_words(raw, name):
            dealt = sb.tile([P, 2 * S], U8, name=name, align_bytes=64)
            nc.vector.tensor_copy(
                out=dealt[:].rearrange("p (t m b) -> p t m b", t=PACK, b=2),
                in_=raw[:].rearrange("p (m t b) -> p t m b", t=PACK, b=2),
            )
            return dealt

        def deal_scales(raw, name):
            dealt = sb.tile([P, S], U8, name=name, align_bytes=64)
            nc.vector.tensor_copy(
                out=dealt[:].rearrange("p (t m) -> p t m", t=PACK),
                in_=raw[:].rearrange("p (m t) -> p t m", t=PACK),
            )
            return dealt

        def entries(list_tile, a, b):
            return list_tile[:, a // 16 : b // 16]

        offs_sb = lists.tile([P, S // 16], U16, name="offs_sb")
        n1_sb = lists.tile([P, S // 16], U16, name="n1_sb")
        n2_sb = lists.tile([P, S // 16], U16, name="n2_sb")
        n3_sb = lists.tile([P, S // 16], U16, name="n3_sb")
        xw = sb.tile([P, T], I32, name="xw", align_bytes=64)
        xs = sb.tile([P, T], U8, name="xs", align_bytes=64)
        w1w = sb.tile([P, 2 * S], U8, name="w1w", align_bytes=64)
        w1s = sb.tile([P, S], U8, name="w1s", align_bytes=64)
        gain = sb.tile([P, PACK], F32, name="gain")
        one = sb.tile([P, 1], F32, name="one")
        warm = sb.tile([P, 1], F32, name="warm")

        w2w = sb.tile([P, 2 * S], U8, name="w2w", align_bytes=64)
        w2s = sb.tile([P, S], U8, name="w2s", tag="w2s_then_part", align_bytes=64)
        nc.vector.memset(xs[:].bitcast(I32), 0)
        nc.vector.memset(w1s[:].bitcast(I32), 0)
        nc.vector.memset(one[:], 1.0)
        nc.vector.memset(w2s[:].bitcast(I32), 0)

        x_rows = x_words[0].rearrange("p n t -> p (n t)").bitcast(I32)
        nc.sync.dma_start(offs_sb[:], offs)
        nc.scalar.dma_start(out=w1w[:].bitcast(I32), in_=w1_words[0].bitcast(I32))
        nc.sync.dma_start(n2_sb[:], n2)
        load_scale_rows([nc.sync, nc.scalar] * 2, xs, x_scales)
        nc.sync.dma_start(out=xw[:, 0:X_FIRST], in_=x_rows[:, 0:X_FIRST])
        load_scale_rows([nc.sync] * 4, w1s, w1_scales)
        nc.sync.dma_start(out=xw[:, X_FIRST:T], in_=x_rows[:, X_FIRST:T])
        nc.scalar.activation(warm[:], one[:], ACT.Sqrt)
        nc.sync.dma_start(out=w2w[:].bitcast(I32), in_=w2_words[0].bitcast(I32))
        load_scale_rows([nc.sync] * 4, w2s, w2_scales)
        nc.sync.dma_start(n1_sb[:], n1)
        nc.sync.dma_start(n3_sb[:], n3)
        nc.sync.dma_start(out=gain[:], in_=gn.rearrange("(p t) o -> p (t o)", t=PACK))

        w1_codes = deal_words(w1w, "w1_codes")
        picked_scales = sb.tile([P, S], U8, name="picked_scales", align_bytes=64)
        nc.vector.tensor_copy(picked_scales[:], xs[:].indirect(offs_sb[:]))
        w1_bytes = deal_scales(w1s, "w1_bytes")
        picked_words = sb.tile([P, S], I32, name="picked_words", align_bytes=64)
        for a, b in HALVES:
            nc.vector.tensor_copy(picked_words[:, a:b].bitcast(U32), xw[:].bitcast(U32).indirect(entries(offs_sb, a, b)))
        w2_codes = deal_words(w2w, "w2_codes")
        w2_bytes = deal_scales(w2s, "w2_bytes")

        def product(out, codes, scale_bytes, t, rhs, rhs_scale):
            nc.tensor.matmul_mx(
                out=out,
                lhsT=codes[:, 2 * P * t : 2 * P * (t + 1)].bitcast(FP4X4),
                lhsT_scale=scale_bytes[:, P * t : P * (t + 1)],
                rhs=rhs.bitcast(FP8X4),
                rhs_scale=rhs_scale,
                start=True,
                stop=True,
            )

        part = sb.tile([P, PACK, S], F32, name="part", tag="w2s_then_part", align_bytes=64)
        total = sb.tile([P, PACK, S], F32, name="total", tag="total_then_gate")
        root = sb.tile([P, PACK, S], F32, name="root")
        own = sb.tile([P, PACK, S], F32, name="own")
        z_codes = sb.tile([P, S], I32, name="z_codes", align_bytes=64)
        z_scales = sb.tile([P, S], U8, name="z_scales", align_bytes=64)
        h_win = [sb.tile([P, S], F32, name=f"h_win{t}") for t in range(PACK)]
        h_own = sb.tile([P, PACK, S], F32, name="h_own")

        z_planes = sb.tile([P, PACK, S], BF16, name="z_planes", align_bytes=64)

        def woven(tile, a, b):
            return tile[:, PACK * a : PACK * b].rearrange("p (c i t) -> p c t i", i=4, t=PACK)

        def by_plane(tile, a, b):
            return tile[:, :, a:b].rearrange("p t (c i) -> p c t i", i=4)

        half = S // 2
        windows = []
        for t in range(PACK):
            sq1 = sb.tile([P, S], F32, name=f"sq1_{t}")
            sq2 = sb.tile([P, S], F32, name=f"sq2_{t}")
            for a, b in HALVES if t == 0 else ((0, S),):
                y = psum.tile([P, b - a], F32, name=f"y{t}_{a}", tag=f"bank{t + (b == S)}")
                product(y[:], w1_codes, w1_bytes, t, picked_words[:, a:b], picked_scales[:, a:b])
                nc.scalar.activation(sq1[:, a:b], y[:], ACT.Square)
                nc.scalar.activation(own[:, t, a:b], y[:], ACT.Square, scale=2.0)
            if t == 0:
                nc.scalar.activation(sq2[:], sq1[:], ACT.Copy, scale=2.0)
            else:
                nc.scalar.activation(sq2[:], y[:], ACT.Square, scale=2.0**0.5)
            windows.append((sq1, sq2))

        for t in range(PACK):
            sq1, sq2 = windows[t]
            for a, b in HALVES:
                nc.vector.tensor_tensor(part[:, t, a:b], sq1[:].indirect(entries(n2_sb, a, b)), own[:, t, a:b], ALU.add)
            for a, b in HALVES:
                nc.vector.tensor_tensor(total[:, t, a:b], sq2[:].indirect(entries(n1_sb, a, b)), part[:, t, a:b], ALU.add)

        def take_root(t0, t1, a, b):
            nc.scalar.activation(root[:, t0:t1, a:b], total[:, t0:t1, a:b], ACT.Sqrt, scale=0.25, bias=0.1)

        def gain_on_scalar(t, a, b):
            nc.scalar.activation(z_planes[:, t, a:b], root[:, t, a:b], ACT.Copy, scale=gain[:, t : t + 1])

        def gain_on_vector(t, a, b):
            nc.vector.tensor_scalar(z_planes[:, t, a:b], root[:, t, a:b], gain[:, t : t + 1], None, ALU.mult)

        take_root(0, 2, 0, S)
        take_root(2, 3, 0, S)
        gain_on_scalar(0, 0, half)
        gain_on_scalar(1, 0, half)
        gain_on_vector(2, 0, half)
        take_root(3, 4, 0, half)
        gain_on_vector(3, 0, half)
        gain_on_scalar(0, half, S)
        gain_on_scalar(1, half, S)
        take_root(3, 4, half, S)
        gain_on_scalar(2, half, S)
        gain_on_vector(3, half, S)

        gate = sb.tile([P, PACK, S], F32, name="gate", tag="total_then_gate")
        nc.scalar.activation(gate[:, 0, 0:1], one[:], ACT.Sigmoid)

        quarter = S // 4
        for a in range(0, S, quarter):
            b = a + quarter
            z_bf = sb.tile([P, quarter * PACK], BF16, name="z_bf", bufs=2, align_bytes=64)
            nc.vector.tensor_copy(woven(z_bf, 0, quarter), by_plane(z_planes, a, b))
            nc.vector.quantize_mx(out=z_codes[:, a:b].bitcast(FP8X4), scales=z_scales[:, a:b], in_=z_bf[:])

        def second_product(out, t, a, b):
            product(out, w2_codes, w2_bytes, t, z_codes[:, a:b], z_scales[:, a:b])

        first = psum.tile([P, 2, half], F32, name="h_first", tag="bank5")
        for t in (0, 1):
            second_product(first[:, t, :], t, 0, half)
        nc.vector.tensor_copy(h_win[0][:, 0:half], first[:, 0, :])
        nc.vector.tensor_copy(h_own[:, 0:2, 0:half], first[:])
        nc.vector.tensor_copy(h_win[1][:, 0:half], first[:, 1, :])
        for t in range(PACK):
            a = half if t < 2 else 0
            bank = psum.tile([P, S - a], F32, name=f"h_rest{t}", tag=f"bank{(6 + t) % 8}")
            second_product(bank[:], t, a, S)
            nc.scalar.copy(h_win[t][:, a:S], bank[:])
            nc.sync.dma_start(out=h_own[:, t, half:S], in_=h_win[t][:, half:S])
            if t >= 2:
                nc.scalar.copy(h_own[:, t, 0:half], bank[:, 0:half])
        for a, b in SLICES:
            nc.scalar.activation(gate[:, :, a:b], h_own[:, :, a:b], ACT.Sigmoid)

        diff = sb.tile([P, PACK, S], F32, name="diff")
        res = sb.tile([P, PACK, S], F32, name="res")
        res_bf = sb.tile([P, S * PACK], BF16, name="res_bf", align_bytes=64)
        res_codes = sb.tile([P, S], I32, name="res_codes", align_bytes=64)
        res_scales = sb.tile([P, S], U8, name="res_scales", align_bytes=64)
        out_rows = out_0.rearrange("(p t) j -> p t j", t=PACK)
        out_words = out_1[0].rearrange("p j t -> p (j t)").bitcast(I32)
        for a, b in SLICES:
            for t in range(PACK):
                nc.vector.tensor_tensor(diff[:, t, a:b], h_win[t][:].indirect(entries(n3_sb, a, b)), h_own[:, t, a:b], ALU.subtract)
            pieces = ((a, b),) if b < S else ((a, (a + b) // 2), ((a + b) // 2, b))
            for c, d in pieces:
                nc.vector.scalar_tensor_tensor(res[:, :, c:d], diff[:, :, c:d], -1.0, gate[:, :, c:d], ALU.mult, ALU.mult)
            nc.sync.dma_start(out=out_rows[:, :, a:b], in_=res[:, :, a:b])
            if b < S:
                nc.scalar.copy(
                    res_bf[:, PACK * a : PACK * b].rearrange("p (j t) -> p j t", t=PACK),
                    res[:, :, a:b].rearrange("p t j -> p j t"),
                )
            else:
                for c, d in pieces:
                    nc.vector.tensor_copy(woven(res_bf, c, d), by_plane(res, c, d))
            nc.vector.quantize_mx(out=res_codes[:, a:b].bitcast(FP8X4), scales=res_scales[:, a:b], in_=res_bf[:, PACK * a : PACK * b])
            nc.sync.dma_start(out=out_words[:, a:b], in_=res_codes[:, a:b])
        for q in range(4):
            queue = nc.sync if q % 2 else nc.scalar
            queue.dma_start(out=out_2[0, 4 * q : 4 * q + 4, :].bitcast(I32), in_=res_scales[32 * q : 32 * q + 4, :].bitcast(I32))
